import numpy as np
import ml_dtypes


def mxq(x, axis, fmt="e4m3"):
    dtype, down = {"e4m3": (ml_dtypes.float8_e4m3fn, 7), "e5m2": (ml_dtypes.float8_e5m2, 14)}[fmt]
    v = np.moveaxis(np.asarray(x, np.float32).astype(ml_dtypes.bfloat16).astype(np.float64), axis, -1)
    blocks = v.reshape(v.shape[:-1] + (-1, 32))
    amax = np.abs(blocks).max(-1, keepdims=True)
    byte = np.maximum(np.where(amax > 0, np.frexp(amax)[1] - 1 + 127, 0) - down, 1)
    scale = np.exp2(byte - 127.0)
    codes = (blocks / scale).astype(np.float32).astype(dtype).astype(np.float64)
    return np.moveaxis((codes * scale).reshape(v.shape), -1, axis)


WIDE = False


def mx_kscale(k):
    if not WIDE:
        return np.ones(k)
    levels = np.array([10, -10, 5, -5, 0])
    if k % 512:
        return np.exp2(np.random.permutation(np.resize(levels, k // 32))).repeat(32)
    a = np.empty((k // 512, 16))
    for p in range(k // 512):
        a[p, :8] = np.random.permutation(np.resize(levels, 8))
        for g in range(8):
            far = levels[np.abs(levels - a[p, g]) >= 10]
            a[p, g + 8] = far[np.random.randint(len(far))]
    return np.exp2(a.ravel()).repeat(32)


def f64(x):
    return np.asarray(x).astype(np.float64)


def striped(idx):
    return np.tile(idx.reshape(-1, 16).T, (8, 1)).astype(np.uint16)


def unstriped(offs):
    return offs[:16].T.reshape(-1).astype(np.int64)


E2M1 = np.array([0.0, 0.5, 1.0, 1.5, 2.0, 3.0, 4.0, 6.0, -0.0, -0.5, -1.0, -1.5, -2.0, -3.0, -4.0, -6.0])


def pack_weight(w, fmt):
    k, n = w.shape
    w = f64(np.asarray(w, np.float32).astype(ml_dtypes.bfloat16)).reshape(k // 32, 32, n)
    amax = np.abs(w).max(1)
    if fmt == "e4m3":
        byte = np.frexp(amax)[1] - 1 + 127 - 7
    else:
        mant, ex = np.frexp(amax / 6.0)
        byte = np.where(mant > 0.5, ex, ex - 1) + 127
    byte = np.clip(np.where(amax > 0, byte, 1), 1, 254)
    scaled = (w * np.exp2(127.0 - byte)[:, None, :]).reshape(k, n).astype(np.float32)
    by_word = np.ascontiguousarray(scaled.reshape(k // 512, 128, 4, n).transpose(0, 1, 3, 2))
    if fmt == "e4m3":
        words = by_word.astype(ml_dtypes.float8_e4m3fn).view(np.uint8)
    else:
        c = by_word.astype(ml_dtypes.float4_e2m1fn).view(np.uint8) & 0xF
        words = (c[..., 0::2] | (c[..., 1::2] << 4)).reshape(k // 512, 128, 2 * n)
    return np.ascontiguousarray(words), np.ascontiguousarray(byte.astype(np.uint8).reshape(k // 512, 16, n))


def unpack_weight(words, scales, fmt):
    g, _, n = scales.shape
    words = np.ascontiguousarray(words).reshape(g, 128, n, -1)
    if fmt == "e4m3":
        vals = words.view(ml_dtypes.float8_e4m3fn).astype(np.float64)
    else:
        nib = np.empty((g, 128, n, 4), np.uint8)
        nib[..., 0::2] = words & 0xF
        nib[..., 1::2] = words >> 4
        vals = E2M1[nib]
    vals = vals * np.repeat(np.exp2(scales.astype(np.float64) - 127.0), 8, axis=1)[..., None]
    return vals.transpose(0, 1, 3, 2).reshape(g * 512, n)


def gelu(v):
    return 0.5 * v * (1.0 + np.tanh(np.sqrt(2.0 / np.pi) * (v + 0.044715 * v**3)))


K, H, N, T, S, T2, P = 1024, 1024, 768, 4096, 1024, 2048, 1024


def setup_inputs():
    n = np.random.standard_normal
    s = mx_kscale(K)[:, None]
    u = mx_kscale(H)[:, None]
    d = {}
    d["tab_words"], d["tab_scales"] = pack_weight(n((K, T)) * s, "e4m3")
    d["offs"] = striped(np.random.permutation(T)[:S])
    d["offs2"] = striped(np.random.permutation(T2)[:S])
    d["offs3"] = striped(np.random.permutation(T2)[:P])
    d["offs4"] = striped(np.random.permutation(T2)[:P])
    d["w1_words"], d["w1_scales"] = pack_weight(1.5 * n((K, H)) / K**0.5 / s, "e2m1")
    d["b1"] = (0.9 * n(H)).astype(np.float32)
    d["gain"] = (1.2 * np.exp(0.3 * n(H)) * u[:, 0]).astype(np.float32)
    d["wgs"] = np.exp(0.3 * n((128, S))).astype(np.float32)
    d["page0"] = (0.9 * n((H, T2)) * u).astype(np.float32)
    d["lo"] = ((0.4 * n(H) - 0.2) * u[:, 0]).astype(np.float32)
    d["w2"] = (3.5 * n((H, N)) / H**0.5 / u).astype(np.float32)
    d["wgo"] = np.exp(0.3 * n((128, P))).astype(np.float32)
    d["page1"] = np.random.uniform(0.0, 1.0, (N, T2)).astype(np.float32)
    return d


def reference(tab_words, tab_scales, offs, offs2, offs3, offs4, w1_words, w1_scales, b1, gain, wgs, page0, lo, w2, wgo, page1):
    v = unpack_weight(tab_words, tab_scales, "e4m3")[:, unstriped(offs)]
    w1 = unpack_weight(w1_words, w1_scales, "e2m1")
    h = f64(gain)[:, None] * np.tanh((w1.T @ v) + f64(b1)[:, None])
    page = f64(page0).copy()
    page[:, unstriped(offs2)] = np.tile(f64(wgs), (H // 128, 1)) * h
    x = np.maximum(page[:, unstriped(offs3)], f64(lo)[:, None])
    e = mxq(f64(w2), 0, "e4m3").T @ mxq(x, 0, "e4m3")
    y = 1.0 / (1.0 + np.exp(-e))
    out = f64(page1).copy()
    out[:, unstriped(offs4)] = np.tile(f64(wgo), (N // 128, 1)) * y
    return out

@@ -1,0 +1,253 @@
+from contextlib import ExitStack
+
+import concourse.mybir as mybir
+
+K, H, N, T, S, T2, PICKS = 1024, 1024, 768, 4096, 1024, 2048, 1024
+FLOPS = 2 * K * H * S + 2 * H * N * PICKS
+
+F32 = mybir.dt.float32
+BF16 = mybir.dt.bfloat16
+I32 = mybir.dt.int32
+U32 = mybir.dt.uint32
+U16 = mybir.dt.uint16
+U8 = mybir.dt.uint8
+FP8X4 = mybir.dt.float8_e4m3fn_x4
+FP4X4 = mybir.dt.float4_e2m1fn_x4
+ACT = mybir.ActivationFunctionType
+ALU = mybir.AluOpType
+
+P = 128
+PACK = 4
+PASS = P * PACK
+QUADS = 4
+HALF = 512
+PER_COL = 16
+KIB = 1024
+F32_MAX = 3.4028234663852886e38
+W2_COLS = 384
+SPLIT_TILES = 3
+
+
+def entries(offsets, first, count):
+    return offsets[:, first // PER_COL : (first + count) // PER_COL]
+
+
+def load_scale_rows(queue, planes, scales):
+    for q in range(QUADS):
+        queue.dma_start(
+            out=planes[32 * q : 32 * q + 4, :, :].bitcast(I32),
+            in_=scales[:, 4 * q : 4 * q + 4, :].rearrange("a r c -> r a c").bitcast(I32),
+        )
+
+
+def tile_list_fogger_page_refresh_kernel(
+    tc, tab_words, tab_scales, offs, offs2, offs3, offs4, w1_words, w1_scales, b1, gain, wgs, page0, lo, w2, wgo, page1, out
+):
+    nc = tc.nc
+    k_passes = K // PASS
+    r_passes = H // PASS
+    halves = S // HALF
+    n_tiles = N // P
+
+    with ExitStack() as ctx:
+        lists = ctx.enter_context(tc.tile_pool(name="lists", bufs=1))
+        keep = ctx.enter_context(tc.tile_pool(name="keep", bufs=1))
+        shared = ctx.enter_context(tc.tile_pool(name="shared", bufs=1))
+        ring = ctx.enter_context(tc.tile_pool(name="ring", bufs=2))
+        psum = ctx.enter_context(tc.psum_pool(name="psum", bufs=4))
+
+        def load_list(name, src):
+            tile = lists.tile([P, S // PER_COL], U16, name=name)
+            nc.sync.dma_start(tile[:], src)
+            return tile
+
+        def load_channels(name, src):
+            tile = keep.tile([P, r_passes, PACK], F32, name=name)
+            nc.sync.dma_start(out=tile[:], in_=src.rearrange("(b p t) -> p b t", p=P, t=PACK))
+            return tile
+
+        tab_planes = keep.tile([P, k_passes, T], U8)
+        nc.vector.memset(tab_planes[:, 0, :].bitcast(I32), 0)
+        nc.gpsimd.memset(tab_planes[:, 1, :].bitcast(I32), 0)
+        w1_planes_raw = keep.tile([P, k_passes, H], U8)
+        nc.gpsimd.memset(w1_planes_raw[:].rearrange("p a c -> p (a c)").bitcast(I32), 0)
+        load_scale_rows(nc.gpsimd, w1_planes_raw, w1_scales)
+
+        table = [shared.tile([P, T], I32, name=f"table{a}", offset=16 * KIB * a) for a in range(k_passes)]
+
+        def load_table(a):
+            nc.sync.dma_start(out=table[a][:], in_=tab_words[a].rearrange("p t i -> p (t i)").bitcast(I32))
+
+        load_table(0)
+        load_scale_rows(nc.sync, tab_planes, tab_scales)
+        idx = load_list("idx", offs)
+        w1_raw = keep.tile([P, k_passes, H // 2], I32)
+        nc.sync.dma_start(out=w1_raw[:], in_=w1_words.rearrange("a p c -> p a c").bitcast(I32))
+        load_table(1)
+        idx2 = load_list("idx2", offs2)
+        b1_sb = load_channels("b1_sb", b1)
+        gain_sb = load_channels("gain_sb", gain)
+
+        wgs_rows = wgs.rearrange("(q t) j -> q t j", t=PACK)
+        wgs_first = shared.tile([P, 1, S], F32, offset=32 * KIB)
+        wgs_rest = shared.tile([P, PACK - 1, S], F32, offset=36 * KIB)
+
+        def load_wgs(tile, t0, t1):
+            for q in range(QUADS):
+                nc.sync.dma_start(out=tile[32 * q : 32 * q + 32, :, :], in_=wgs_rows[:, t0:t1, :])
+
+        page_rows = page0.rearrange("(b p t) c -> b t p c", p=P, t=PACK)
+        pages = {}
+
+        def load_page(b, t):
+            pages[b, t] = keep.tile([P, T2], F32, name=f"page{b}{t}")
+            nc.sync.dma_start(out=pages[b, t][:], in_=page_rows[b, t])
+
+        load_wgs(wgs_first, 0, 1)
+        for b in range(r_passes):
+            load_page(b, 0)
+        load_wgs(wgs_rest, 1, PACK)
+        for t in range(1, PACK):
+            for b in range(r_passes):
+                load_page(b, t)
+        idx3 = load_list("idx3", offs3)
+        lo_sb = load_channels("lo_sb", lo)
+
+        v_words, v_scales, w1_codes, w1_planes = [], [], [], []
+        for a in range(k_passes):
+            w1_codes.append(keep.tile([P, H], U16, name=f"w1_codes{a}", align_bytes=64))
+            w1_planes.append(keep.tile([P, H], U8, name=f"w1_planes{a}", align_bytes=64))
+        for b in range(r_passes):
+            cols = slice(PASS * b, PASS * (b + 1))
+            for a in range(k_passes):
+                nc.scalar.copy(
+                    out=w1_codes[a][:, cols].rearrange("p (t c i) -> p c t i", t=PACK, i=8),
+                    in_=w1_raw[:, a, :].bitcast(U16)[:, cols].rearrange("p (c i t) -> p c t i", t=PACK, i=8),
+                )
+                nc.gpsimd.tensor_copy(
+                    out=w1_planes[a][:, cols].rearrange("p (t c i) -> p c t i", t=PACK, i=16),
+                    in_=w1_planes_raw[:, a, cols].rearrange("p (c i t) -> p c t i", t=PACK, i=16),
+                )
+        for a in range(k_passes):
+            picked = keep.tile([P, S], U32, name=f"v_words{a}", align_bytes=64)
+            step = HALF if a == k_passes - 1 else S
+            for j0 in range(0, S, step):
+                nc.vector.tensor_copy(picked[:, j0 : j0 + step], table[a][:].bitcast(U32).indirect(entries(idx, j0, step)))
+            v_words.append(picked)
+            if a == 0:
+                for c in range(k_passes):
+                    rows = keep.tile([P, S], U8, name=f"v_scales{c}", align_bytes=64)
+                    nc.vector.tensor_copy(rows[:], tab_planes[:, c, :].indirect(idx[:]))
+                    v_scales.append(rows)
+
+        for t in range(PACK):
+            weights = wgs_first[:, 0, :] if t == 0 else wgs_rest[:, t - 1, :]
+            for b in range(r_passes):
+                rows = slice(PASS * b + P * t, PASS * b + P * (t + 1))
+                h = ring.tile([P, S], F32, tag="factor", bufs=4)
+                step = HALF if (t, b) == (0, 0) else S
+                for u in range(halves):
+                    cols = slice(HALF * u, HALF * (u + 1))
+                    acc = psum.tile([P, HALF], F32, tag="acc1")
+                    for a in range(k_passes):
+                        nc.tensor.matmul_mx(
+                            out=acc[:],
+                            lhsT=w1_codes[a][:, rows].bitcast(FP4X4),
+                            lhsT_scale=w1_planes[a][:, rows],
+                            rhs=v_words[a][:, cols].bitcast(FP8X4),
+                            rhs_scale=v_scales[a][:, cols],
+                            start=(a == 0),
+                            stop=(a == k_passes - 1),
+                        )
+                    squashed = ring.tile([P, HALF], F32)
+                    nc.scalar.activation(out=squashed[:], in_=acc[:], func=ACT.Tanh, bias=b1_sb[:, b, t : t + 1])
+                    nc.scalar.activation(out=h[:, cols], in_=squashed[:], func=ACT.Copy, scale=gain_sb[:, b, t : t + 1])
+                for j0 in range(0, S, step):
+                    nc.vector.tensor_tensor(
+                        pages[b, t][:].indirect(entries(idx2, j0, step)),
+                        h[:, j0 : j0 + step],
+                        weights[:, j0 : j0 + step],
+                        ALU.mult,
+                    )
+
+        w2_codes, w2_planes = [], []
+        for b in range(r_passes):
+            codes = keep.tile([P, N], U32, name=f"w2_codes{b}", align_bytes=64)
+            plane = keep.tile([P, N], U8, name=f"w2_planes{b}", align_bytes=64)
+            for n0 in range(0, N, W2_COLS):
+                cols = slice(n0, n0 + W2_COLS)
+                w2_raw = ring.tile([P, PACK, W2_COLS], F32)
+                nc.sync.dma_start(
+                    out=w2_raw[:], in_=w2[PASS * b : PASS * (b + 1), cols].rearrange("(p t) n -> p t n", t=PACK)
+                )
+                w2_woven = ring.tile([P, W2_COLS, PACK], BF16, align_bytes=64)
+                nc.scalar.copy(
+                    out=w2_woven[:].rearrange("p (c i) t -> p c t i", i=4),
+                    in_=w2_raw[:].rearrange("p t (c i) -> p c t i", i=4),
+                )
+                nc.vector.quantize_mx(
+                    out=codes[:, cols].bitcast(FP8X4), scales=plane[:, cols], in_=w2_woven[:].rearrange("p n t -> p (n t)")
+                )
+            w2_codes.append(codes)
+            w2_planes.append(plane)
+
+        wgo_sb = keep.tile([P, PICKS], F32)
+        nc.sync.dma_start(out=wgo_sb[:], in_=wgo)
+        idx4 = load_list("idx4", offs4)
+        foggers = []
+        for n in range(n_tiles):
+            tile = shared.tile([P, T2], F32, name=f"fogger{n}", offset=8 * KIB * n)
+            nc.sync.dma_start(out=tile[:], in_=page1[P * n : P * (n + 1), :])
+            foggers.append(tile)
+
+        x_codes, x_planes = {}, {}
+        for u in range(halves):
+            for b in range(r_passes):
+                x_rows = ring.tile([P, PACK, HALF], BF16)
+                for t in range(PACK):
+                    recalled = ring.tile([P, HALF], F32, bufs=4)
+                    nc.vector.tensor_copy(recalled[:], pages[b, t][:].indirect(entries(idx3, HALF * u, HALF)))
+                    nc.gpsimd.tensor_scalar(
+                        x_rows[:, t, :], recalled[:], F32_MAX, lo_sb[:, b, t : t + 1], ALU.min, ALU.max
+                    )
+                x_woven = ring.tile([P, HALF, PACK], BF16, align_bytes=64)
+                nc.scalar.copy(
+                    out=x_woven[:].rearrange("p (c i) t -> p c t i", i=4),
+                    in_=x_rows[:].rearrange("p t (c i) -> p c t i", i=4),
+                )
+                x_codes[u, b] = keep.tile([P, HALF], U32, name=f"x_codes{u}{b}", align_bytes=64)
+                x_planes[u, b] = keep.tile([P, HALF], U8, name=f"x_planes{u}{b}", align_bytes=64)
+                nc.vector.quantize_mx(
+                    out=x_codes[u, b][:].bitcast(FP8X4),
+                    scales=x_planes[u, b][:],
+                    in_=x_woven[:].rearrange("p j t -> p (j t)"),
+                )
+
+        def refresh(n, j0, count):
+            y = ring.tile([P, count], F32, tag="factor", bufs=4)
+            rows = slice(P * n, P * (n + 1))
+            for c0 in range(0, count, HALF):
+                u = (j0 + c0) // HALF
+                acc = psum.tile([P, HALF], F32, tag="acc2")
+                for b in range(r_passes):
+                    nc.tensor.matmul_mx(
+                        out=acc[:],
+                        lhsT=w2_codes[b][:, rows].bitcast(FP8X4),
+                        lhsT_scale=w2_planes[b][:, rows],
+                        rhs=x_codes[u, b][:].bitcast(FP8X4),
+                        rhs_scale=x_planes[u, b][:],
+                        start=(b == 0),
+                        stop=(b == r_passes - 1),
+                    )
+                nc.scalar.activation(out=y[:, c0 : c0 + HALF], in_=acc[:], func=ACT.Sigmoid)
+            nc.vector.tensor_tensor(
+                foggers[n][:].indirect(entries(idx4, j0, count)), y[:], wgo_sb[:, j0 : j0 + count], ALU.mult
+            )
+            if j0 + count == PICKS:
+                nc.sync.dma_start(out=out[rows, :], in_=foggers[n][:])
+
+        for u in range(halves):
+            for n in range(SPLIT_TILES):
+                refresh(n, HALF * u, HALF)
+        for n in range(SPLIT_TILES, n_tiles):
+            refresh(n, 0, PICKS)

@@ -23,7 +23,6 @@ QUADS = 4
 HALF = 512
 PER_COL = 16
 KIB = 1024
-F32_MAX = 3.4028234663852886e38
 W2_COLS = 384
 SPLIT_TILES = 3
 
@@ -67,22 +66,22 @@ def tile_list_fogger_page_refresh_kernel(
             return tile
 
         tab_planes = keep.tile([P, k_passes, T], U8)
+        w1_planes_raw = keep.tile([P, k_passes, H], U8)
+        nc.vector.memset(w1_planes_raw[:].rearrange("p a c -> p (a c)").bitcast(I32), 0)
         nc.vector.memset(tab_planes[:, 0, :].bitcast(I32), 0)
         nc.gpsimd.memset(tab_planes[:, 1, :].bitcast(I32), 0)
-        w1_planes_raw = keep.tile([P, k_passes, H], U8)
-        nc.gpsimd.memset(w1_planes_raw[:].rearrange("p a c -> p (a c)").bitcast(I32), 0)
-        load_scale_rows(nc.gpsimd, w1_planes_raw, w1_scales)
 
         table = [shared.tile([P, T], I32, name=f"table{a}", offset=16 * KIB * a) for a in range(k_passes)]
 
         def load_table(a):
             nc.sync.dma_start(out=table[a][:], in_=tab_words[a].rearrange("p t i -> p (t i)").bitcast(I32))
 
-        load_table(0)
-        load_scale_rows(nc.sync, tab_planes, tab_scales)
         idx = load_list("idx", offs)
         w1_raw = keep.tile([P, k_passes, H // 2], I32)
         nc.sync.dma_start(out=w1_raw[:], in_=w1_words.rearrange("a p c -> p a c").bitcast(I32))
+        load_scale_rows(nc.sync, w1_planes_raw, w1_scales)
+        load_scale_rows(nc.sync, tab_planes, tab_scales)
+        load_table(0)
         load_table(1)
         idx2 = load_list("idx2", offs2)
         b1_sb = load_channels("b1_sb", b1)
@@ -124,21 +123,20 @@ def tile_list_fogger_page_refresh_kernel(
                     out=w1_codes[a][:, cols].rearrange("p (t c i) -> p c t i", t=PACK, i=8),
                     in_=w1_raw[:, a, :].bitcast(U16)[:, cols].rearrange("p (c i t) -> p c t i", t=PACK, i=8),
                 )
-                nc.gpsimd.tensor_copy(
+                nc.vector.tensor_copy(
                     out=w1_planes[a][:, cols].rearrange("p (t c i) -> p c t i", t=PACK, i=16),
                     in_=w1_planes_raw[:, a, cols].rearrange("p (c i t) -> p c t i", t=PACK, i=16),
                 )
+        for a in range(k_passes):
+            picked = keep.tile([P, S], U8, name=f"v_scales{a}", align_bytes=64)
+            nc.vector.tensor_copy(picked[:], tab_planes[:, a, :].indirect(idx[:]))
+            v_scales.append(picked)
         for a in range(k_passes):
             picked = keep.tile([P, S], U32, name=f"v_words{a}", align_bytes=64)
             step = HALF if a == k_passes - 1 else S
             for j0 in range(0, S, step):
                 nc.vector.tensor_copy(picked[:, j0 : j0 + step], table[a][:].bitcast(U32).indirect(entries(idx, j0, step)))
             v_words.append(picked)
-            if a == 0:
-                for c in range(k_passes):
-                    rows = keep.tile([P, S], U8, name=f"v_scales{c}", align_bytes=64)
-                    nc.vector.tensor_copy(rows[:], tab_planes[:, c, :].indirect(idx[:]))
-                    v_scales.append(rows)
 
         for t in range(PACK):
             weights = wgs_first[:, 0, :] if t == 0 else wgs_rest[:, t - 1, :]
@@ -200,20 +198,21 @@ def tile_list_fogger_page_refresh_kernel(
             nc.sync.dma_start(out=tile[:], in_=page1[P * n : P * (n + 1), :])
             foggers.append(tile)
 
-        x_codes, x_planes = {}, {}
-        for u in range(halves):
-            for b in range(r_passes):
-                x_rows = ring.tile([P, PACK, HALF], BF16)
-                for t in range(PACK):
-                    recalled = ring.tile([P, HALF], F32, bufs=4)
-                    nc.vector.tensor_copy(recalled[:], pages[b, t][:].indirect(entries(idx3, HALF * u, HALF)))
-                    nc.gpsimd.tensor_scalar(
-                        x_rows[:, t, :], recalled[:], F32_MAX, lo_sb[:, b, t : t + 1], ALU.min, ALU.max
-                    )
+        x_codes, x_planes, x_rows, recalled = {}, {}, {}, {}
+
+        def recall(u, b, t):
+            recalled[u, b, t] = ring.tile([P, HALF], F32, name="recalled", bufs=4)
+            nc.vector.tensor_copy(recalled[u, b, t][:], pages[b, t][:].indirect(entries(idx3, HALF * u, HALF)))
+
+        def bound(u, b, t):
+            if t == 0:
+                x_rows[u, b] = ring.tile([P, PACK, HALF], BF16, name="x_rows")
+            nc.vector.tensor_scalar(x_rows[u, b][:, t, :], recalled[u, b, t][:], lo_sb[:, b, t : t + 1], None, ALU.max)
+            if t == PACK - 1:
                 x_woven = ring.tile([P, HALF, PACK], BF16, align_bytes=64)
                 nc.scalar.copy(
                     out=x_woven[:].rearrange("p (c i) t -> p c t i", i=4),
-                    in_=x_rows[:].rearrange("p t (c i) -> p c t i", i=4),
+                    in_=x_rows[u, b][:].rearrange("p t (c i) -> p c t i", i=4),
                 )
                 x_codes[u, b] = keep.tile([P, HALF], U32, name=f"x_codes{u}{b}", align_bytes=64)
                 x_planes[u, b] = keep.tile([P, HALF], U8, name=f"x_planes{u}{b}", align_bytes=64)
@@ -222,6 +221,13 @@ def tile_list_fogger_page_refresh_kernel(
                     scales=x_planes[u, b][:],
                     in_=x_woven[:].rearrange("p j t -> p (j t)"),
                 )
+
+        steps = [(u, b, t) for u in range(halves) for b in range(r_passes) for t in range(PACK)]
+        for i, step_now in enumerate(steps):
+            recall(*step_now)
+            if i > 0:
+                bound(*steps[i - 1])
+        bound(*steps[-1])
 
         def refresh(n, j0, count):
             y = ring.tile([P, count], F32, tag="factor", bufs=4)

@@ -23,6 +23,7 @@ QUADS = 4
 HALF = 512
 PER_COL = 16
 KIB = 1024
+F32_MAX = 3.4028234663852886e38
 W2_COLS = 384
 SPLIT_TILES = 3
 
@@ -207,7 +208,9 @@ def tile_list_fogger_page_refresh_kernel(
         def bound(u, b, t):
             if t == 0:
                 x_rows[u, b] = ring.tile([P, PACK, HALF], BF16, name="x_rows")
-            nc.vector.tensor_scalar(x_rows[u, b][:, t, :], recalled[u, b, t][:], lo_sb[:, b, t : t + 1], None, ALU.max)
+            nc.gpsimd.tensor_scalar(
+                x_rows[u, b][:, t, :], recalled[u, b, t][:], F32_MAX, lo_sb[:, b, t : t + 1], ALU.min, ALU.max
+            )
             if t == PACK - 1:
                 x_woven = ring.tile([P, HALF, PACK], BF16, align_bytes=64)
                 nc.scalar.copy(

from contextlib import ExitStack

import concourse.mybir as mybir

K, H, N, T, S, T2, PICKS = 1024, 1024, 768, 4096, 1024, 2048, 1024
FLOPS = 2 * K * H * S + 2 * H * N * PICKS

F32 = mybir.dt.float32
BF16 = mybir.dt.bfloat16
I32 = mybir.dt.int32
U32 = mybir.dt.uint32
U16 = mybir.dt.uint16
U8 = mybir.dt.uint8
FP8X4 = mybir.dt.float8_e4m3fn_x4
FP4X4 = mybir.dt.float4_e2m1fn_x4
ACT = mybir.ActivationFunctionType
ALU = mybir.AluOpType

P = 128
PACK = 4
PASS = P * PACK
QUADS = 4
HALF = 512
PER_COL = 16
KIB = 1024
F32_MAX = 3.4028234663852886e38
W2_COLS = 384
SPLIT_TILES = 3


def entries(offsets, first, count):
    return offsets[:, first // PER_COL : (first + count) // PER_COL]


def load_scale_rows(queue, planes, scales):
    for q in range(QUADS):
        queue.dma_start(
            out=planes[32 * q : 32 * q + 4, :, :].bitcast(I32),
            in_=scales[:, 4 * q : 4 * q + 4, :].rearrange("a r c -> r a c").bitcast(I32),
        )


def tile_list_fogger_page_refresh_kernel(
    tc, tab_words, tab_scales, offs, offs2, offs3, offs4, w1_words, w1_scales, b1, gain, wgs, page0, lo, w2, wgo, page1, out
):
    nc = tc.nc
    k_passes = K // PASS
    r_passes = H // PASS
    halves = S // HALF
    n_tiles = N // P

    with ExitStack() as ctx:
        lists = ctx.enter_context(tc.tile_pool(name="lists", bufs=1))
        keep = ctx.enter_context(tc.tile_pool(name="keep", bufs=1))
        shared = ctx.enter_context(tc.tile_pool(name="shared", bufs=1))
        ring = ctx.enter_context(tc.tile_pool(name="ring", bufs=2))
        psum = ctx.enter_context(tc.psum_pool(name="psum", bufs=4))

        def load_list(name, src):
            tile = lists.tile([P, S // PER_COL], U16, name=name)
            nc.sync.dma_start(tile[:], src)
            return tile

        def load_channels(name, src):
            tile = keep.tile([P, r_passes, PACK], F32, name=name)
            nc.sync.dma_start(out=tile[:], in_=src.rearrange("(b p t) -> p b t", p=P, t=PACK))
            return tile

        tab_planes = keep.tile([P, k_passes, T], U8)
        w1_planes_raw = keep.tile([P, k_passes, H], U8)
        nc.vector.memset(w1_planes_raw[:].rearrange("p a c -> p (a c)").bitcast(I32), 0)
        nc.vector.memset(tab_planes[:, 0, :].bitcast(I32), 0)
        nc.gpsimd.memset(tab_planes[:, 1, :].bitcast(I32), 0)

        table = [shared.tile([P, T], I32, name=f"table{a}", offset=16 * KIB * a) for a in range(k_passes)]

        def load_table(a):
            nc.sync.dma_start(out=table[a][:], in_=tab_words[a].rearrange("p t i -> p (t i)").bitcast(I32))

        idx = load_list("idx", offs)
        w1_raw = keep.tile([P, k_passes, H // 2], I32)
        nc.sync.dma_start(out=w1_raw[:], in_=w1_words.rearrange("a p c -> p a c").bitcast(I32))
        load_scale_rows(nc.sync, w1_planes_raw, w1_scales)
        load_scale_rows(nc.sync, tab_planes, tab_scales)
        load_table(0)
        load_table(1)
        idx2 = load_list("idx2", offs2)
        b1_sb = load_channels("b1_sb", b1)
        gain_sb = load_channels("gain_sb", gain)

        wgs_rows = wgs.rearrange("(q t) j -> q t j", t=PACK)
        wgs_first = shared.tile([P, 1, S], F32, offset=32 * KIB)
        wgs_rest = shared.tile([P, PACK - 1, S], F32, offset=36 * KIB)

        def load_wgs(tile, t0, t1):
            for q in range(QUADS):
                nc.sync.dma_start(out=tile[32 * q : 32 * q + 32, :, :], in_=wgs_rows[:, t0:t1, :])

        page_rows = page0.rearrange("(b p t) c -> b t p c", p=P, t=PACK)
        pages = {}

        def load_page(b, t):
            pages[b, t] = keep.tile([P, T2], F32, name=f"page{b}{t}")
            nc.sync.dma_start(out=pages[b, t][:], in_=page_rows[b, t])

        load_wgs(wgs_first, 0, 1)
        for b in range(r_passes):
            load_page(b, 0)
        load_wgs(wgs_rest, 1, PACK)
        for t in range(1, PACK):
            for b in range(r_passes):
                load_page(b, t)
        idx3 = load_list("idx3", offs3)
        lo_sb = load_channels("lo_sb", lo)

        v_words, v_scales, w1_codes, w1_planes = [], [], [], []
        for a in range(k_passes):
            w1_codes.append(keep.tile([P, H], U16, name=f"w1_codes{a}", align_bytes=64))
            w1_planes.append(keep.tile([P, H], U8, name=f"w1_planes{a}", align_bytes=64))
        for b in range(r_passes):
            cols = slice(PASS * b, PASS * (b + 1))
            for a in range(k_passes):
                nc.scalar.copy(
                    out=w1_codes[a][:, cols].rearrange("p (t c i) -> p c t i", t=PACK, i=8),
                    in_=w1_raw[:, a, :].bitcast(U16)[:, cols].rearrange("p (c i t) -> p c t i", t=PACK, i=8),
                )
                nc.vector.tensor_copy(
                    out=w1_planes[a][:, cols].rearrange("p (t c i) -> p c t i", t=PACK, i=16),
                    in_=w1_planes_raw[:, a, cols].rearrange("p (c i t) -> p c t i", t=PACK, i=16),
                )
        for a in range(k_passes):
            picked = keep.tile([P, S], U8, name=f"v_scales{a}", align_bytes=64)
            nc.vector.tensor_copy(picked[:], tab_planes[:, a, :].indirect(idx[:]))
            v_scales.append(picked)
        for a in range(k_passes):
            picked = keep.tile([P, S], U32, name=f"v_words{a}", align_bytes=64)
            step = HALF if a == k_passes - 1 else S
            for j0 in range(0, S, step):
                nc.vector.tensor_copy(picked[:, j0 : j0 + step], table[a][:].bitcast(U32).indirect(entries(idx, j0, step)))
            v_words.append(picked)

        for t in range(PACK):
            weights = wgs_first[:, 0, :] if t == 0 else wgs_rest[:, t - 1, :]
            for b in range(r_passes):
                rows = slice(PASS * b + P * t, PASS * b + P * (t + 1))
                h = ring.tile([P, S], F32, tag="factor", bufs=4)
                step = HALF if (t, b) == (0, 0) else S
                for u in range(halves):
                    cols = slice(HALF * u, HALF * (u + 1))
                    acc = psum.tile([P, HALF], F32, tag="acc1")
                    for a in range(k_passes):
                        nc.tensor.matmul_mx(
                            out=acc[:],
                            lhsT=w1_codes[a][:, rows].bitcast(FP4X4),
                            lhsT_scale=w1_planes[a][:, rows],
                            rhs=v_words[a][:, cols].bitcast(FP8X4),
                            rhs_scale=v_scales[a][:, cols],
                            start=(a == 0),
                            stop=(a == k_passes - 1),
                        )
                    squashed = ring.tile([P, HALF], F32)
                    nc.scalar.activation(out=squashed[:], in_=acc[:], func=ACT.Tanh, bias=b1_sb[:, b, t : t + 1])
                    nc.scalar.activation(out=h[:, cols], in_=squashed[:], func=ACT.Copy, scale=gain_sb[:, b, t : t + 1])
                for j0 in range(0, S, step):
                    nc.vector.tensor_tensor(
                        pages[b, t][:].indirect(entries(idx2, j0, step)),
                        h[:, j0 : j0 + step],
                        weights[:, j0 : j0 + step],
                        ALU.mult,
                    )

        w2_codes, w2_planes = [], []
        for b in range(r_passes):
            codes = keep.tile([P, N], U32, name=f"w2_codes{b}", align_bytes=64)
            plane = keep.tile([P, N], U8, name=f"w2_planes{b}", align_bytes=64)
            for n0 in range(0, N, W2_COLS):
                cols = slice(n0, n0 + W2_COLS)
                w2_raw = ring.tile([P, PACK, W2_COLS], F32)
                nc.sync.dma_start(
                    out=w2_raw[:], in_=w2[PASS * b : PASS * (b + 1), cols].rearrange("(p t) n -> p t n", t=PACK)
                )
                w2_woven = ring.tile([P, W2_COLS, PACK], BF16, align_bytes=64)
                nc.scalar.copy(
                    out=w2_woven[:].rearrange("p (c i) t -> p c t i", i=4),
                    in_=w2_raw[:].rearrange("p t (c i) -> p c t i", i=4),
                )
                nc.vector.quantize_mx(
                    out=codes[:, cols].bitcast(FP8X4), scales=plane[:, cols], in_=w2_woven[:].rearrange("p n t -> p (n t)")
                )
            w2_codes.append(codes)
            w2_planes.append(plane)

        wgo_sb = keep.tile([P, PICKS], F32)
        nc.sync.dma_start(out=wgo_sb[:], in_=wgo)
        idx4 = load_list("idx4", offs4)
        foggers = []
        for n in range(n_tiles):
            tile = shared.tile([P, T2], F32, name=f"fogger{n}", offset=8 * KIB * n)
            nc.sync.dma_start(out=tile[:], in_=page1[P * n : P * (n + 1), :])
            foggers.append(tile)

        x_codes, x_planes, x_rows, recalled = {}, {}, {}, {}

        def recall(u, b, t):
            recalled[u, b, t] = ring.tile([P, HALF], F32, name="recalled", bufs=4)
            nc.vector.tensor_copy(recalled[u, b, t][:], pages[b, t][:].indirect(entries(idx3, HALF * u, HALF)))

        def bound(u, b, t):
            if t == 0:
                x_rows[u, b] = ring.tile([P, PACK, HALF], BF16, name="x_rows")
            nc.gpsimd.tensor_scalar(
                x_rows[u, b][:, t, :], recalled[u, b, t][:], F32_MAX, lo_sb[:, b, t : t + 1], ALU.min, ALU.max
            )
            if t == PACK - 1:
                x_woven = ring.tile([P, HALF, PACK], BF16, align_bytes=64)
                nc.scalar.copy(
                    out=x_woven[:].rearrange("p (c i) t -> p c t i", i=4),
                    in_=x_rows[u, b][:].rearrange("p t (c i) -> p c t i", i=4),
                )
                x_codes[u, b] = keep.tile([P, HALF], U32, name=f"x_codes{u}{b}", align_bytes=64)
                x_planes[u, b] = keep.tile([P, HALF], U8, name=f"x_planes{u}{b}", align_bytes=64)
                nc.vector.quantize_mx(
                    out=x_codes[u, b][:].bitcast(FP8X4),
                    scales=x_planes[u, b][:],
                    in_=x_woven[:].rearrange("p j t -> p (j t)"),
                )

        steps = [(u, b, t) for u in range(halves) for b in range(r_passes) for t in range(PACK)]
        for i, step_now in enumerate(steps):
            recall(*step_now)
            if i > 0:
                bound(*steps[i - 1])
        bound(*steps[-1])

        def refresh(n, j0, count):
            y = ring.tile([P, count], F32, tag="factor", bufs=4)
            rows = slice(P * n, P * (n + 1))
            for c0 in range(0, count, HALF):
                u = (j0 + c0) // HALF
                acc = psum.tile([P, HALF], F32, tag="acc2")
                for b in range(r_passes):
                    nc.tensor.matmul_mx(
                        out=acc[:],
                        lhsT=w2_codes[b][:, rows].bitcast(FP8X4),
                        lhsT_scale=w2_planes[b][:, rows],
                        rhs=x_codes[u, b][:].bitcast(FP8X4),
                        rhs_scale=x_planes[u, b][:],
                        start=(b == 0),
                        stop=(b == r_passes - 1),
                    )
                nc.scalar.activation(out=y[:, c0 : c0 + HALF], in_=acc[:], func=ACT.Sigmoid)
            nc.vector.tensor_tensor(
                foggers[n][:].indirect(entries(idx4, j0, count)), y[:], wgo_sb[:, j0 : j0 + count], ALU.mult
            )
            if j0 + count == PICKS:
                nc.sync.dma_start(out=out[rows, :], in_=foggers[n][:])

        for u in range(halves):
            for n in range(SPLIT_TILES):
                refresh(n, HALF * u, HALF)
        for n in range(SPLIT_TILES, n_tiles):
            refresh(n, 0, PICKS)
